import numpy as np
import ml_dtypes

BF16 = ml_dtypes.bfloat16


def bf(x):
    return np.asarray(x, np.float32).astype(BF16)


def f32(x):
    return np.asarray(x, np.float32)


def f64(x):
    return np.asarray(x).astype(np.float64)


def striped(idx):
    return np.tile(idx.reshape(-1, 16).T, (8, 1))


S, K, M, N = 256, 128, 256, 256


def setup_inputs():
    return {"base": bf(np.random.standard_normal((M, S))), "x": bf(np.random.standard_normal((K, N))), "w": bf(np.random.standard_normal((K, M)) / np.sqrt(K)), "b": f32(0.5 * np.random.standard_normal((M, 1))), "offs": striped(np.random.permutation(S))}


def reference(base, x, w, b, offs):
    idx = offs[:16].T.reshape(-1)
    z = f64(base).copy()
    z[:, idx] += f64(w).T @ f64(x)
    return z + f64(b)

@@ -1,0 +1,60 @@
+import concourse.mybir as mybir
+from concourse.masks import make_identity
+
+BF16, F32, U16 = mybir.dt.bfloat16, mybir.dt.float32, mybir.dt.uint16
+
+P = 128
+TOKENS = 256
+ENTRIES = 256
+FEATURES = 256
+BLOCKS = FEATURES // P
+
+FLOPS = 2 * P * FEATURES * ENTRIES
+
+
+def tile_scatter_matmul_kernel(tc, base, x, w, b, offs, out):
+    nc = tc.nc
+    base_blocks = base.rearrange("(a p) t -> p a t", p=P)
+    out_blocks = out.rearrange("(a p) t -> p a t", p=P)
+
+    with (
+        tc.tile_pool(name="held", bufs=1) as held,
+        tc.psum_pool(name="windows", bufs=1) as windows,
+    ):
+        offsets = held.tile([P, ENTRIES // 16], U16, name="offsets")
+        nc.sync.dma_start(offsets[:], offs)
+
+        base_sb = held.tile([P, BLOCKS, TOKENS], BF16, name="base_sb")
+        nc.scalar.dma_start(base_sb[:], base_blocks)
+        x_sb = held.tile([P, ENTRIES], BF16, name="x_sb")
+        nc.sync.dma_start(x_sb[:], x)
+        w_sb = held.tile([P, FEATURES], BF16, name="w_sb")
+        nc.sync.dma_start(w_sb[:], w)
+        bias_sb = held.tile([P, BLOCKS], F32, name="bias_sb")
+        with nc.allow_non_contiguous_dma(reason="one float32 of the bias to a partition"):
+            nc.scalar.dma_start(bias_sb[:], b.rearrange("(a p) o -> p (a o)", p=P))
+
+        identity = held.tile([P, P], BF16, name="identity")
+        make_identity(nc, identity[:])
+
+        window = [windows.tile([P, TOKENS], F32, name=f"window{a}") for a in range(BLOCKS)]
+
+        for a in range(BLOCKS):
+            nc.tensor.matmul(window[a][:], identity[:], base_sb[:, a, :], start=True, stop=False)
+
+        for a in range(BLOCKS):
+            nc.tensor.matmul(
+                window[a][:].indirect(offsets[:]),
+                w_sb[:, a * P : (a + 1) * P],
+                x_sb[:],
+                start=False,
+                stop=True,
+            )
+
+        result = held.tile([P, BLOCKS, TOKENS], F32, name="result")
+        nc.vector.tensor_scalar_add(result[:, 0, :], window[0][:], bias_sb[:, 0:1])
+        nc.sync.dma_start(out_blocks[:, 0, :], result[:, 0, :])
+        nc.scalar.activation(
+            result[:, 1, :], window[1][:], mybir.ActivationFunctionType.Identity, bias=bias_sb[:, 1:2]
+        )
+        nc.scalar.dma_start(out_blocks[:, 1, :], result[:, 1, :])

@@ -8,6 +8,9 @@ TOKENS = 256
 ENTRIES = 256
 FEATURES = 256
 BLOCKS = FEATURES // P
+BANK = 512
+
+WARMING_MATMULS = 2 * 1024 // BANK
 
 FLOPS = 2 * P * FEATURES * ENTRIES
 
@@ -36,6 +39,12 @@ def tile_scatter_matmul_kernel(tc, base, x, w, b, offs, out):
 
         identity = held.tile([P, P], BF16, name="identity")
         make_identity(nc, identity[:])
+
+        zeros = held.tile([P, BANK], BF16, name="zeros")
+        nc.vector.memset(zeros[:], 0.0)
+        unread = windows.tile([P, BANK], F32, name="unread")
+        for i in range(WARMING_MATMULS):
+            nc.tensor.matmul(unread[:], zeros[:, 0:P], zeros[:], start=True, stop=True)
 
         window = [windows.tile([P, TOKENS], F32, name=f"window{a}") for a in range(BLOCKS)]
 

@@ -8,9 +8,6 @@ TOKENS = 256
 ENTRIES = 256
 FEATURES = 256
 BLOCKS = FEATURES // P
-BANK = 512
-
-WARMING_MATMULS = 2 * 1024 // BANK
 
 FLOPS = 2 * P * FEATURES * ENTRIES
 
@@ -40,11 +37,9 @@ def tile_scatter_matmul_kernel(tc, base, x, w, b, offs, out):
         identity = held.tile([P, P], BF16, name="identity")
         make_identity(nc, identity[:])
 
-        zeros = held.tile([P, BANK], BF16, name="zeros")
-        nc.vector.memset(zeros[:], 0.0)
-        unread = windows.tile([P, BANK], F32, name="unread")
-        for i in range(WARMING_MATMULS):
-            nc.tensor.matmul(unread[:], zeros[:, 0:P], zeros[:], start=True, stop=True)
+        primer = held.tile([P, 1], F32, name="primer")
+        nc.vector.memset(primer[:], 0.0)
+        nc.scalar.activation(primer[:], primer[:], mybir.ActivationFunctionType.Identity)
 
         window = [windows.tile([P, TOKENS], F32, name=f"window{a}") for a in range(BLOCKS)]
 

@@ -8,6 +8,9 @@ TOKENS = 256
 ENTRIES = 256
 FEATURES = 256
 BLOCKS = FEATURES // P
+BANK = 512
+
+WARMING_MATMULS = 3 * 1024 // (2 * BANK)
 
 FLOPS = 2 * P * FEATURES * ENTRIES
 
@@ -25,14 +28,27 @@ def tile_scatter_matmul_kernel(tc, base, x, w, b, offs, out):
         nc.sync.dma_start(offsets[:], offs)
 
         base_sb = held.tile([P, BLOCKS, TOKENS], BF16, name="base_sb")
-        nc.scalar.dma_start(base_sb[:], base_blocks)
+        nc.scalar.dma_start(base_sb[:, 0, :], base_blocks[:, 0, :])
+        nc.sync.dma_start(base_sb[:, 1, :], base_blocks[:, 1, :])
         x_sb = held.tile([P, ENTRIES], BF16, name="x_sb")
         nc.sync.dma_start(x_sb[:], x)
         w_sb = held.tile([P, FEATURES], BF16, name="w_sb")
-        nc.sync.dma_start(w_sb[:], w)
+        nc.scalar.dma_start(w_sb[:], w)
         bias_sb = held.tile([P, BLOCKS], F32, name="bias_sb")
         with nc.allow_non_contiguous_dma(reason="one float32 of the bias to a partition"):
             nc.scalar.dma_start(bias_sb[:], b.rearrange("(a p) o -> p (a o)", p=P))
+
+        zeros = held.tile([P, P], BF16, name="zeros")
+        nc.gpsimd.memset(zeros[:], 0.0)
+        unread = windows.tile([P, BANK // P, P], F32, name="unread")
+        for i in range(WARMING_MATMULS):
+            nc.tensor.matmul(
+                unread[:],
+                zeros[:],
+                zeros[:].unsqueeze(1).to_broadcast([P, BANK // P, P]),
+                start=True,
+                stop=True,
+            )
 
         identity = held.tile([P, P], BF16, name="identity")
         make_identity(nc, identity[:])

@@ -24,16 +24,15 @@ def tile_scatter_matmul_kernel(tc, base, x, w, b, offs, out):
         tc.tile_pool(name="held", bufs=1) as held,
         tc.psum_pool(name="windows", bufs=1) as windows,
     ):
-        offsets = held.tile([P, ENTRIES // 16], U16, name="offsets")
-        nc.sync.dma_start(offsets[:], offs)
-
         base_sb = held.tile([P, BLOCKS, TOKENS], BF16, name="base_sb")
-        nc.scalar.dma_start(base_sb[:, 0, :], base_blocks[:, 0, :])
-        nc.sync.dma_start(base_sb[:, 1, :], base_blocks[:, 1, :])
+        nc.sync.dma_start(base_sb[:, 0, :], base_blocks[:, 0, :])
+        nc.scalar.dma_start(base_sb[:, 1, :], base_blocks[:, 1, :])
         x_sb = held.tile([P, ENTRIES], BF16, name="x_sb")
         nc.sync.dma_start(x_sb[:], x)
         w_sb = held.tile([P, FEATURES], BF16, name="w_sb")
         nc.scalar.dma_start(w_sb[:], w)
+        offsets = held.tile([P, ENTRIES // 16], U16, name="offsets")
+        nc.sync.dma_start(offsets[:], offs)
         bias_sb = held.tile([P, BLOCKS], F32, name="bias_sb")
         with nc.allow_non_contiguous_dma(reason="one float32 of the bias to a partition"):
             nc.scalar.dma_start(bias_sb[:], b.rearrange("(a p) o -> p (a o)", p=P))

@@ -9,6 +9,7 @@ ENTRIES = 256
 FEATURES = 256
 BLOCKS = FEATURES // P
 BANK = 512
+SQUARE = 32
 
 WARMING_MATMULS = 3 * 1024 // (2 * BANK)
 
@@ -33,9 +34,14 @@ def tile_scatter_matmul_kernel(tc, base, x, w, b, offs, out):
         nc.scalar.dma_start(w_sb[:], w)
         offsets = held.tile([P, ENTRIES // 16], U16, name="offsets")
         nc.sync.dma_start(offsets[:], offs)
-        bias_sb = held.tile([P, BLOCKS], F32, name="bias_sb")
-        with nc.allow_non_contiguous_dma(reason="one float32 of the bias to a partition"):
-            nc.scalar.dma_start(bias_sb[:], b.rearrange("(a p) o -> p (a o)", p=P))
+        bias_rows = held.tile([P, P], F32, name="bias_rows", align_bytes=64)
+        nc.vector.memset(bias_rows[:], 0.0)
+        nc.scalar.dma_start(
+            bias_rows[0:P:SQUARE, 0 : BLOCKS * SQUARE].rearrange("q (a i) -> q a i", a=BLOCKS),
+            b.rearrange("(a q i) o -> q a (i o)", a=BLOCKS, i=SQUARE),
+        )
+        bias_cols = held.tile([P, P], F32, name="bias_cols", align_bytes=64)
+        nc.vector.transpose(bias_cols[:], bias_rows[:])
 
         zeros = held.tile([P, P], BF16, name="zeros")
         nc.gpsimd.memset(zeros[:], 0.0)
@@ -71,9 +77,9 @@ def tile_scatter_matmul_kernel(tc, base, x, w, b, offs, out):
             )
 
         result = held.tile([P, BLOCKS, TOKENS], F32, name="result")
-        nc.vector.tensor_scalar_add(result[:, 0, :], window[0][:], bias_sb[:, 0:1])
+        nc.vector.tensor_scalar_add(result[:, 0, :], window[0][:], bias_cols[:, 0:1])
         nc.sync.dma_start(out_blocks[:, 0, :], result[:, 0, :])
         nc.scalar.activation(
-            result[:, 1, :], window[1][:], mybir.ActivationFunctionType.Identity, bias=bias_sb[:, 1:2]
+            result[:, 1, :], window[1][:], mybir.ActivationFunctionType.Identity, bias=bias_cols[:, SQUARE : SQUARE + 1]
         )
         nc.scalar.dma_start(out_blocks[:, 1, :], result[:, 1, :])

import concourse.mybir as mybir
from concourse.masks import make_identity

BF16, F32, U16 = mybir.dt.bfloat16, mybir.dt.float32, mybir.dt.uint16

P = 128
TOKENS = 256
ENTRIES = 256
FEATURES = 256
BLOCKS = FEATURES // P
BANK = 512
SQUARE = 32

WARMING_MATMULS = 3 * 1024 // (2 * BANK)

FLOPS = 2 * P * FEATURES * ENTRIES


def tile_scatter_matmul_kernel(tc, base, x, w, b, offs, out):
    nc = tc.nc
    base_blocks = base.rearrange("(a p) t -> p a t", p=P)
    out_blocks = out.rearrange("(a p) t -> p a t", p=P)

    with (
        tc.tile_pool(name="held", bufs=1) as held,
        tc.psum_pool(name="windows", bufs=1) as windows,
    ):
        base_sb = held.tile([P, BLOCKS, TOKENS], BF16, name="base_sb")
        nc.sync.dma_start(base_sb[:, 0, :], base_blocks[:, 0, :])
        nc.scalar.dma_start(base_sb[:, 1, :], base_blocks[:, 1, :])
        x_sb = held.tile([P, ENTRIES], BF16, name="x_sb")
        nc.sync.dma_start(x_sb[:], x)
        w_sb = held.tile([P, FEATURES], BF16, name="w_sb")
        nc.scalar.dma_start(w_sb[:], w)
        offsets = held.tile([P, ENTRIES // 16], U16, name="offsets")
        nc.sync.dma_start(offsets[:], offs)
        bias_rows = held.tile([P, P], F32, name="bias_rows", align_bytes=64)
        nc.vector.memset(bias_rows[:], 0.0)
        nc.scalar.dma_start(
            bias_rows[0:P:SQUARE, 0 : BLOCKS * SQUARE].rearrange("q (a i) -> q a i", a=BLOCKS),
            b.rearrange("(a q i) o -> q a (i o)", a=BLOCKS, i=SQUARE),
        )
        bias_cols = held.tile([P, P], F32, name="bias_cols", align_bytes=64)
        nc.vector.transpose(bias_cols[:], bias_rows[:])

        zeros = held.tile([P, P], BF16, name="zeros")
        nc.gpsimd.memset(zeros[:], 0.0)
        unread = windows.tile([P, BANK // P, P], F32, name="unread")
        for i in range(WARMING_MATMULS):
            nc.tensor.matmul(
                unread[:],
                zeros[:],
                zeros[:].unsqueeze(1).to_broadcast([P, BANK // P, P]),
                start=True,
                stop=True,
            )

        identity = held.tile([P, P], BF16, name="identity")
        make_identity(nc, identity[:])

        primer = held.tile([P, 1], F32, name="primer")
        nc.vector.memset(primer[:], 0.0)
        nc.scalar.activation(primer[:], primer[:], mybir.ActivationFunctionType.Identity)

        window = [windows.tile([P, TOKENS], F32, name=f"window{a}") for a in range(BLOCKS)]

        for a in range(BLOCKS):
            nc.tensor.matmul(window[a][:], identity[:], base_sb[:, a, :], start=True, stop=False)

        for a in range(BLOCKS):
            nc.tensor.matmul(
                window[a][:].indirect(offsets[:]),
                w_sb[:, a * P : (a + 1) * P],
                x_sb[:],
                start=False,
                stop=True,
            )

        result = held.tile([P, BLOCKS, TOKENS], F32, name="result")
        nc.vector.tensor_scalar_add(result[:, 0, :], window[0][:], bias_cols[:, 0:1])
        nc.sync.dma_start(out_blocks[:, 0, :], result[:, 0, :])
        nc.scalar.activation(
            result[:, 1, :], window[1][:], mybir.ActivationFunctionType.Identity, bias=bias_cols[:, SQUARE : SQUARE + 1]
        )
        nc.scalar.dma_start(out_blocks[:, 1, :], result[:, 1, :])
